import numpy as np, ml_dtypes
CORES = [33,161,289,417,57,185,313,441]
N = 8
import mx_ref
NC, G = 128, 4
C = np.float32(0.023)
BF = ml_dtypes.bfloat16
def cut(t, i, w=512):
    return t[:, w * i:w * i + w]
def tile(rs):
    return np.stack(rs, axis=2).reshape(128, -1).astype(BF)
def layer(w, X):
    out = []
    for i in range(G):
        for t in range(len(X)):
            p = mx_ref.matmul(mx_ref.quantize(cut(w, len(X) * i + t)), X[t])
            z = p if t == 0 else z + p
        out.append(z)
    return out
def act(Z):
    return [np.maximum(z, 0) * C for z in Z]
def setup_inputs(rng):
    def f(*shape):
        return mx_ref.flush((rng.standard_normal(shape, dtype=np.float32) * np.exp2(rng.integers(-2, 3, shape[:-1] + (1,)))).astype(BF))
    return {"x": f(N, 128, 4 * NC), "w1": f(N, 128, G * 512), "w2": f(N, 128, 512)}
def setup_inputs_blocks(rng):
    d = setup_inputs(rng)
    for k in ("x", "w1", "w2"): d[k] = mx_ref.spread(d[k], rng, 2)
    return d
def setup_inputs_wide(rng):
    d = setup_inputs(rng)
    for k in ("x", "w1", "w2"): d[k] = mx_ref.flush((d[k].astype(np.float32) * np.exp2(rng.integers(-6, 7, (N, 1, 1))).astype(np.float32)).astype(BF))
    return d
def reference(x, w1, w2):
    X = [mx_ref.quantize(x[j]) for j in range(N)]
    y = np.zeros((N, 128, NC), np.float32)
    for c in range(N):
        for r in range(N):
            p = mx_ref.matmul(mx_ref.quantize(w2[r]), mx_ref.quantize(tile(act(layer(w1[r], [X[c]])))))
            y[c] = p if r == 0 else y[c] + p
    return {"y": y}

@@ -1,0 +1,219 @@
+from concourse.bass import DstId, RemoteDMATransfer
+from concourse.mybir import dt, AluOpType, ActivationFunctionType
+
+N = 8
+NC = 128
+G = 4
+BLK = (G + 1) * NC
+PIECES = (("codes", 0, 2 * NC), ("plane", 0, BLK), ("codes", 2 * NC, BLK))
+SCALE = 0.023
+RING = 7
+
+SCRATCH = {
+    "wb": ("sbuf", [128, 4 * BLK], "bfloat16"),
+    "xb": ("sbuf", [128, 4 * NC], "bfloat16"),
+    "wq": ("sbuf", [128, N * BLK], "float8_e4m3fn_x4"),
+    "ws": ("sbuf", [128, N * BLK], "uint8"),
+    "xq": ("sbuf", [128, NC], "float8_e4m3fn_x4"),
+    "xs": ("sbuf", [128, NC], "uint8"),
+    "h": ("sbuf", [128, N * 4 * NC], "bfloat16"),
+    "hq": ("sbuf", [128, N * NC], "float8_e4m3fn_x4"),
+    "hs": ("sbuf", [128, N * NC], "uint8"),
+    "ysb": ("sbuf", [128, NC], "float32"),
+    "z": ("psum", [128, 512 * (RING + 1)], "float32"),
+}
+SEMAPHORES = (["a%d_%d" % (r, k) for r in range(N) for k in range(len(PIECES))]
+              + ["zb%d" % j for j in range(RING)] + ["ab%d" % j for j in range(RING)]
+              + ["qh%d" % r for r in range(N)]
+              + ["ld0", "ld1", "ldx", "q0", "q1", "qx", "ys", "yc", "st", "sent"])
+
+
+def _bits(m):
+    return bin(m).count("1")
+
+
+def _plan(T, topo):
+    ranks = list(T.cores)
+    world = range((max(topo.host(c) for c in ranks) + 1) * topo.CORES_PER_HOST)
+
+    def twin(a):
+        return [b for b in ranks if topo.host(b) == topo.host(a) and topo.chip(b) != topo.chip(a)][0]
+
+    def peers(a):
+        return [b for b in ranks if b != a and topo.chip(b) == topo.chip(a)]
+
+    def near(a):
+        return [b for b in peers(a) if topo.same_plane(a, b)][0]
+
+    def cabled(a):
+        return [b for b in peers(a) if topo.may_write(a, b) and not topo.same_plane(a, b)][0]
+
+    hubs = {}
+    for a in ranks:
+        own = [c for c in world if c != a and topo.host(c) == topo.host(a) and topo.chip(c) == topo.chip(a)
+               and topo.may_write(c, twin(a))]
+        same = [c for c in own if topo.die(c) == topo.die(a)]
+        other = [c for c in own if topo.die(c) != topo.die(a)]
+        hubs[a] = {"home": same[0], "switch": same[1], "cable": other[0]}
+
+    def job(r, src, off, on):
+        m_off = topo.mask(src, off[0])
+        for d in off:
+            m_off &= topo.mask(src, d)
+        parts = [(m_off, off)]
+        if on:
+            parts.append((topo.mask(src, on[0]) & ~m_off, on))
+        return (r, parts)
+
+    jobs = {}
+    for r, a in enumerate(ranks):
+        s, c = near(a), cabled(a)
+        jobs[a] = job(r, a, [hubs[c]["cable"], hubs[s]["switch"]], [hubs[a]["home"]])
+        jobs[hubs[a]["home"]] = job(r, hubs[a]["home"], [twin(a), twin(s)], [])
+        jobs[hubs[c]["cable"]] = job(r, hubs[c]["cable"], [twin(c), twin(near(c))], [c])
+        jobs[hubs[s]["switch"]] = job(r, hubs[s]["switch"], [cabled(s)], [s])
+    lands = {}
+    for src in jobs:
+        r, parts = jobs[src]
+        for m, dsts in parts:
+            for d in dsts:
+                lands[(d, r)] = _bits(m)
+
+    def orders(a):
+        s, c = near(a), cabled(a)
+        d = near(c)
+        first = [c, twin(c), twin(a), s, d, twin(d), twin(s)]
+        second = [twin(a), c, twin(c), twin(s), twin(d), s, d]
+        return [ranks.index(b) for b in first], [ranks.index(b) for b in second]
+
+    return jobs, lands, orders
+
+
+def _view(T, r, k):
+    kind, lo, hi = PIECES[k]
+    if kind == "codes":
+        return T.wq[:, BLK * r + lo:BLK * r + hi].bitcast(dt.uint8)
+    return T.ws[:, BLK * r + lo:BLK * r + hi]
+
+
+def _forward(g, core, T, topo, job, k):
+    r, parts = job
+    trs = []
+    for m, dsts in parts:
+        ids = []
+        for d in dsts:
+            rid, pid = topo.addr(d, core)
+            ids.append(DstId(rid=rid, pnc=pid))
+        trs.append(RemoteDMATransfer(dst_ids=ids, dma_engine_mask=m, remote_sem=T.sem["a%d_%d" % (r, k)],
+                                     srcs=[_view(T, r, k)], dsts=[_view(T, r, k) for d in dsts]))
+    g.remote_dma_fused(trs, local_sem=T.sem.sent)
+    return sum(_bits(m) for m, dsts in parts)
+
+
+def rank_program(g, core, T, topo):
+    jobs, lands, orders = _plan(T, topo)
+    if core not in jobs:
+        return
+    me = T.rank_of(core)
+    job = jobs[core]
+    sent = 0
+
+    if me is None:
+        r = job[0]
+        for k in range(len(PIECES)):
+            g.wait_ge(T.sem["a%d_%d" % (r, k)], lands[(core, r)])
+            sent += _forward(g, core, T, topo, job, k)
+        g.wait_ge(T.sem.sent, sent)
+        return
+
+    half = 4 * 2 * NC
+    g.sync.dma_start(T.wb[:, 0:half], T.w1[:, 0:half]).then_inc(T.sem.ld0, 16)
+    g.scalar.dma_start(T.wb[:, half:2 * half], T.w1[:, half:2 * half]).then_inc(T.sem.ld1, 16)
+    g.sync.dma_start(T.wb[:, 2 * half:4 * BLK], T.w2[:, :]).then_inc(T.sem.ld1, 16)
+    g.scalar.dma_start(T.xb[:, :], T.x[:, :]).then_inc(T.sem.ldx, 16)
+
+    s0 = BLK * me
+    g.vector.wait_ge(T.sem.ld0, 16)
+    g.vector.quantize_mx(T.wq[:, s0:s0 + 2 * NC], T.ws[:, s0:s0 + 2 * NC], T.wb[:, 0:half]).then_inc(T.sem.q0, 1)
+    g.vector.wait_ge(T.sem.ld1, 32)
+    g.vector.quantize_mx(T.wq[:, s0 + 2 * NC:s0 + BLK], T.ws[:, s0 + 2 * NC:s0 + BLK],
+                         T.wb[:, half:4 * BLK]).then_inc(T.sem.q1, 1)
+    g.vector.wait_ge(T.sem.ldx, 16)
+    g.vector.quantize_mx(T.xq[:, :], T.xs[:, :], T.xb[:, :]).then_inc(T.sem.qx, 1)
+
+    g.wait_ge(T.sem.q0, 1)
+    sent += _forward(g, core, T, topo, job, 0)
+    g.wait_ge(T.sem.q1, 1)
+    sent += _forward(g, core, T, topo, job, 1)
+    sent += _forward(g, core, T, topo, job, 2)
+
+    zc, ac, turn = [0] * RING, [0] * RING, [0]
+    need = dict((r, []) for r in range(N))
+    ybank = T.z[:, 512 * RING:512 * RING + NC]
+
+    def first_layer(r, i):
+        j = turn[0] % RING
+        turn[0] += 1
+        bank = T.z[:, 512 * j:512 * j + NC]
+        if ac[j]:
+            g.tensor.wait_ge(T.sem["ab%d" % j], ac[j])
+        c0 = BLK * r + NC * i
+        g.tensor.matmul_mx(bank, T.wq[:, c0:c0 + NC], T.ws[:, c0:c0 + NC], T.xq[:, :], T.xs[:, :],
+                           True, True).then_inc(T.sem["zb%d" % j], 1)
+        zc[j] += 1
+        out = T.h[:, 4 * NC * r + i:4 * NC * (r + 1):4]
+        if i % 2 == 0:
+            g.vector.wait_ge(T.sem["zb%d" % j], zc[j])
+            g.vector.tensor_scalar(out, bank, 0.0, SCALE, AluOpType.max, AluOpType.mult).then_inc(T.sem["ab%d" % j], 1)
+        else:
+            g.scalar.wait_ge(T.sem["zb%d" % j], zc[j])
+            g.scalar.activation(out, bank, ActivationFunctionType.Relu, scale=SCALE).then_inc(T.sem["ab%d" % j], 1)
+        ac[j] += 1
+        need[r].append((j, ac[j]))
+
+    def pack(r):
+        for j, n in need[r]:
+            g.vector.wait_ge(T.sem["ab%d" % j], n)
+        g.vector.quantize_mx(T.hq[:, NC * r:NC * (r + 1)], T.hs[:, NC * r:NC * (r + 1)],
+                             T.h[:, 4 * NC * r:4 * NC * (r + 1)]).then_inc(T.sem["qh%d" % r], 1)
+
+    done = [0]
+
+    def second_layer(r):
+        g.tensor.wait_ge(T.sem["qh%d" % r], 1)
+        c0 = BLK * r + G * NC
+        g.tensor.matmul_mx(ybank, T.wq[:, c0:c0 + NC], T.ws[:, c0:c0 + NC], T.hq[:, NC * r:NC * (r + 1)],
+                           T.hs[:, NC * r:NC * (r + 1)], done[0] == 0, done[0] == N - 1).then_inc(T.sem.ys, 1)
+        done[0] += 1
+
+    g.tensor.wait_ge(T.sem.q0, 1)
+    g.tensor.wait_ge(T.sem.q1, 1)
+    g.tensor.wait_ge(T.sem.qx, 1)
+    for i in range(G):
+        first_layer(me, i)
+    pack(me)
+    second_layer(me)
+
+    early, late = orders(core)
+    for r in early:
+        g.tensor.wait_ge(T.sem["a%d_0" % r], lands[(core, r)])
+        g.tensor.wait_ge(T.sem["a%d_1" % r], lands[(core, r)])
+        first_layer(r, 0)
+        first_layer(r, 1)
+    behind = None
+    for r in late:
+        g.tensor.wait_ge(T.sem["a%d_2" % r], lands[(core, r)])
+        first_layer(r, 2)
+        first_layer(r, 3)
+        pack(r)
+        if behind is not None:
+            second_layer(behind)
+        behind = r
+    second_layer(behind)
+
+    g.vector.wait_ge(T.sem.ys, N)
+    g.vector.tensor_copy(T.ysb[:, :], ybank).then_inc(T.sem.yc, 1)
+    g.sync.wait_ge(T.sem.yc, 1)
+    g.sync.dma_start(T.y[:, :], T.ysb[:, :]).then_inc(T.sem.st, 16)
+    g.sync.wait_ge(T.sem.st, 16)
+    g.wait_ge(T.sem.sent, sent)

@@ -5,7 +5,7 @@ N = 8
 NC = 128
 G = 4
 BLK = (G + 1) * NC
-PIECES = (("codes", 0, 2 * NC), ("plane", 0, BLK), ("codes", 2 * NC, BLK))
+PIECES = (("codes", 0, 2 * NC, "A"), ("plane", 0, BLK, "B"), ("codes", 2 * NC, 4 * NC, "B"), ("codes", 4 * NC, BLK, "A"))
 SCALE = 0.023
 RING = 7
 
@@ -54,52 +54,53 @@ def _plan(T, topo):
                and topo.may_write(c, twin(a))]
         same = [c for c in own if topo.die(c) == topo.die(a)]
         other = [c for c in own if topo.die(c) != topo.die(a)]
-        hubs[a] = {"home": same[0], "switch": same[1], "cable": other[0]}
+        hubs[a] = {"homeA": same[0], "cableA": same[1], "homeB": other[0], "cableB": other[1]}
 
-    def job(r, src, off, on):
+    def parts(src, off, on):
         m_off = topo.mask(src, off[0])
         for d in off:
             m_off &= topo.mask(src, d)
-        parts = [(m_off, off)]
+        out = [(m_off, off)]
         if on:
-            parts.append((topo.mask(src, on[0]) & ~m_off, on))
-        return (r, parts)
+            out.append((topo.mask(src, on[0]) & ~m_off, on))
+        return out
 
     jobs = {}
     for r, a in enumerate(ranks):
         s, c = near(a), cabled(a)
-        jobs[a] = job(r, a, [hubs[c]["cable"], hubs[s]["switch"]], [hubs[a]["home"]])
-        jobs[hubs[a]["home"]] = job(r, hubs[a]["home"], [twin(a), twin(s)], [])
-        jobs[hubs[c]["cable"]] = job(r, hubs[c]["cable"], [twin(c), twin(near(c))], [c])
-        jobs[hubs[s]["switch"]] = job(r, hubs[s]["switch"], [cabled(s)], [s])
+        d = near(c)
+        jobs[a] = (r, [(k, parts(a, [hubs[c]["cable" + p[3]]], [hubs[a]["home" + p[3]]])) for k, p in enumerate(PIECES)])
+        for side in "AB":
+            mine = [k for k, p in enumerate(PIECES) if p[3] == side]
+            hh, hc = hubs[a]["home" + side], hubs[c]["cable" + side]
+            jobs[hh] = (r, [(k, parts(hh, [twin(a), s, twin(s)], [])) for k in mine])
+            jobs[hc] = (r, [(k, parts(hc, [twin(c), d, twin(d)], [c])) for k in mine])
     lands = {}
     for src in jobs:
-        r, parts = jobs[src]
-        for m, dsts in parts:
-            for d in dsts:
-                lands[(d, r)] = _bits(m)
+        r, todo = jobs[src]
+        for k, ps in todo:
+            for m, dsts in ps:
+                for d in dsts:
+                    lands[(d, r, k)] = _bits(m)
 
-    def orders(a):
-        s, c = near(a), cabled(a)
+    def order(v):
+        s, c = near(v), cabled(v)
         d = near(c)
-        first = [c, twin(c), twin(a), s, d, twin(d), twin(s)]
-        second = [twin(a), c, twin(c), twin(s), twin(d), s, d]
-        return [ranks.index(b) for b in first], [ranks.index(b) for b in second]
+        return [ranks.index(b) for b in (c, twin(v), twin(c), s, d, twin(s), twin(d))]
 
-    return jobs, lands, orders
+    return jobs, lands, order
 
 
 def _view(T, r, k):
-    kind, lo, hi = PIECES[k]
+    kind, lo, hi = PIECES[k][0:3]
     if kind == "codes":
         return T.wq[:, BLK * r + lo:BLK * r + hi].bitcast(dt.uint8)
     return T.ws[:, BLK * r + lo:BLK * r + hi]
 
 
-def _forward(g, core, T, topo, job, k):
-    r, parts = job
+def _forward(g, core, T, topo, r, k, ps):
     trs = []
-    for m, dsts in parts:
+    for m, dsts in ps:
         ids = []
         for d in dsts:
             rid, pid = topo.addr(d, core)
@@ -107,22 +108,21 @@ def _forward(g, core, T, topo, job, k):
         trs.append(RemoteDMATransfer(dst_ids=ids, dma_engine_mask=m, remote_sem=T.sem["a%d_%d" % (r, k)],
                                      srcs=[_view(T, r, k)], dsts=[_view(T, r, k) for d in dsts]))
     g.remote_dma_fused(trs, local_sem=T.sem.sent)
-    return sum(_bits(m) for m, dsts in parts)
+    return sum(_bits(m) for m, dsts in ps)
 
 
 def rank_program(g, core, T, topo):
-    jobs, lands, orders = _plan(T, topo)
+    jobs, lands, order = _plan(T, topo)
     if core not in jobs:
         return
     me = T.rank_of(core)
-    job = jobs[core]
+    blk, todo = jobs[core]
     sent = 0
 
     if me is None:
-        r = job[0]
-        for k in range(len(PIECES)):
-            g.wait_ge(T.sem["a%d_%d" % (r, k)], lands[(core, r)])
-            sent += _forward(g, core, T, topo, job, k)
+        for k, ps in todo:
+            g.wait_ge(T.sem["a%d_%d" % (blk, k)], lands[(core, blk, k)])
+            sent += _forward(g, core, T, topo, blk, k, ps)
         g.wait_ge(T.sem.sent, sent)
         return
 
@@ -142,14 +142,17 @@ def rank_program(g, core, T, topo):
     g.vector.quantize_mx(T.xq[:, :], T.xs[:, :], T.xb[:, :]).then_inc(T.sem.qx, 1)
 
     g.wait_ge(T.sem.q0, 1)
-    sent += _forward(g, core, T, topo, job, 0)
-    g.wait_ge(T.sem.q1, 1)
-    sent += _forward(g, core, T, topo, job, 1)
-    sent += _forward(g, core, T, topo, job, 2)
+    for k, ps in todo:
+        if k == 1:
+            g.wait_ge(T.sem.q1, 1)
+        sent += _forward(g, core, T, topo, blk, k, ps)
 
     zc, ac, turn = [0] * RING, [0] * RING, [0]
     need = dict((r, []) for r in range(N))
     ybank = T.z[:, 512 * RING:512 * RING + NC]
+
+    def landed(r, k):
+        g.tensor.wait_ge(T.sem["a%d_%d" % (r, k)], lands[(core, r, k)])
 
     def first_layer(r, i):
         j = turn[0] % RING
@@ -180,6 +183,8 @@ def rank_program(g, core, T, topo):
     done = [0]
 
     def second_layer(r):
+        if r != me:
+            landed(r, 3)
         g.tensor.wait_ge(T.sem["qh%d" % r], 1)
         c0 = BLK * r + G * NC
         g.tensor.matmul_mx(ybank, T.wq[:, c0:c0 + NC], T.ws[:, c0:c0 + NC], T.hq[:, NC * r:NC * (r + 1)],
@@ -194,15 +199,14 @@ def rank_program(g, core, T, topo):
     pack(me)
     second_layer(me)
 
-    early, late = orders(core)
-    for r in early:
-        g.tensor.wait_ge(T.sem["a%d_0" % r], lands[(core, r)])
-        g.tensor.wait_ge(T.sem["a%d_1" % r], lands[(core, r)])
+    for r in order(core):
+        landed(r, 0)
+        landed(r, 1)
         first_layer(r, 0)
         first_layer(r, 1)
     behind = None
-    for r in late:
-        g.tensor.wait_ge(T.sem["a%d_2" % r], lands[(core, r)])
+    for r in order(core):
+        landed(r, 2)
         first_layer(r, 2)
         first_layer(r, 3)
         pack(r)

@@ -5,8 +5,14 @@ N = 8
 NC = 128
 G = 4
 BLK = (G + 1) * NC
-PIECES = (("codes", 0, 2 * NC, "A"), ("plane", 0, BLK, "B"), ("codes", 2 * NC, 4 * NC, "B"), ("codes", 4 * NC, BLK, "A"))
+PIECES = (("codes", 0, NC, "A"), ("codes", NC, 2 * NC, "B"), ("codes", 2 * NC, 3 * NC, "B"), ("plane", 0, BLK, "A"),
+          ("codes", 3 * NC, 4 * NC, "B"), ("codes", 4 * NC, BLK, "A"))
+EARLY = 2
+READY = ("q0", "q0", "qm", "q1", "q1", "q1")
+P_TILE = (0, 1, 2, 4)
+P_PLANE, P_W2 = 3, 5
 SCALE = 0.023
+LAG = 2
 RING = 7
 
 SCRATCH = {
@@ -25,11 +31,16 @@ SCRATCH = {
 SEMAPHORES = (["a%d_%d" % (r, k) for r in range(N) for k in range(len(PIECES))]
               + ["zb%d" % j for j in range(RING)] + ["ab%d" % j for j in range(RING)]
               + ["qh%d" % r for r in range(N)]
-              + ["ld0", "ld1", "ldx", "q0", "q1", "qx", "ys", "yc", "st", "sent"])
+              + ["ld0", "ldm", "ld1", "ldx", "q0", "qm", "q1", "qx", "ys", "yc", "st", "sent"])
 
 
 def _bits(m):
     return bin(m).count("1")
+
+
+def _deal(m):
+    one = [1 << i for i in range(m.bit_length()) if (m >> i) & 1]
+    return sum(one[0::2]), sum(one[1::2])
 
 
 def _plan(T, topo):
@@ -56,37 +67,47 @@ def _plan(T, topo):
         other = [c for c in own if topo.die(c) != topo.die(a)]
         hubs[a] = {"homeA": same[0], "cableA": same[1], "homeB": other[0], "cableB": other[1]}
 
-    def parts(src, off, on):
+    def masks(src, off, on):
         m_off = topo.mask(src, off[0])
         for d in off:
             m_off &= topo.mask(src, d)
-        out = [(m_off, off)]
-        if on:
-            out.append((topo.mask(src, on[0]) & ~m_off, on))
-        return out
+        return m_off, topo.mask(src, on) & ~m_off
 
     jobs = {}
     for r, a in enumerate(ranks):
         s, c = near(a), cabled(a)
         d = near(c)
-        jobs[a] = (r, [(k, parts(a, [hubs[c]["cable" + p[3]]], [hubs[a]["home" + p[3]]])) for k, p in enumerate(PIECES)])
+        m_off, m_on = masks(a, [hubs[c]["cableA"], hubs[c]["cableB"]], hubs[a]["homeA"])
+        early = range(EARLY)
+        calls = [[(k, m, [hubs[c]["cable" + PIECES[k][3]]]) for k, m in zip(early, _deal(m_off))],
+                 [(k, m, [hubs[a]["home" + PIECES[k][3]]]) for k, m in zip(early, _deal(m_on))]]
+        for k in range(EARLY, len(PIECES)):
+            side = PIECES[k][3]
+            calls.append([(k, m_off, [hubs[c]["cable" + side]]), (k, m_on, [hubs[a]["home" + side]])])
+        jobs[a] = (r, calls)
         for side in "AB":
             mine = [k for k, p in enumerate(PIECES) if p[3] == side]
             hh, hc = hubs[a]["home" + side], hubs[c]["cable" + side]
-            jobs[hh] = (r, [(k, parts(hh, [twin(a), s, twin(s)], [])) for k in mine])
-            jobs[hc] = (r, [(k, parts(hc, [twin(c), d, twin(d)], [c])) for k in mine])
+            out_h, out_c = [twin(a), s, twin(s)], [twin(c), d, twin(d)]
+            mh = masks(hh, out_h, a)[0]
+            jobs[hh] = (r, [[(k, mh, out_h)] for k in mine])
+            mc_off, mc_on = masks(hc, out_c, c)
+            calls = [[(mine[0], mc_off, out_c)], [(mine[0], mc_on, [c])]]
+            for k in mine[1:]:
+                calls.append([(k, mc_off, out_c), (k, mc_on, [c])])
+            jobs[hc] = (r, calls)
     lands = {}
     for src in jobs:
-        r, todo = jobs[src]
-        for k, ps in todo:
-            for m, dsts in ps:
+        r, calls = jobs[src]
+        for call in calls:
+            for k, m, dsts in call:
                 for d in dsts:
                     lands[(d, r, k)] = _bits(m)
 
     def order(v):
         s, c = near(v), cabled(v)
         d = near(c)
-        return [ranks.index(b) for b in (c, twin(v), twin(c), s, d, twin(s), twin(d))]
+        return [ranks.index(b) for b in (twin(v), s, twin(s), c, twin(c), d, twin(d))]
 
     return jobs, lands, order
 
@@ -98,9 +119,9 @@ def _view(T, r, k):
     return T.ws[:, BLK * r + lo:BLK * r + hi]
 
 
-def _forward(g, core, T, topo, r, k, ps):
+def _forward(g, core, T, topo, r, call):
     trs = []
-    for m, dsts in ps:
+    for k, m, dsts in call:
         ids = []
         for d in dsts:
             rid, pid = topo.addr(d, core)
@@ -108,7 +129,7 @@ def _forward(g, core, T, topo, r, k, ps):
         trs.append(RemoteDMATransfer(dst_ids=ids, dma_engine_mask=m, remote_sem=T.sem["a%d_%d" % (r, k)],
                                      srcs=[_view(T, r, k)], dsts=[_view(T, r, k) for d in dsts]))
     g.remote_dma_fused(trs, local_sem=T.sem.sent)
-    return sum(_bits(m) for m, dsts in ps)
+    return sum(_bits(m) for k, m, dsts in call)
 
 
 def rank_program(g, core, T, topo):
@@ -116,36 +137,46 @@ def rank_program(g, core, T, topo):
     if core not in jobs:
         return
     me = T.rank_of(core)
-    blk, todo = jobs[core]
+    blk, calls = jobs[core]
     sent = 0
 
     if me is None:
-        for k, ps in todo:
-            g.wait_ge(T.sem["a%d_%d" % (blk, k)], lands[(core, blk, k)])
-            sent += _forward(g, core, T, topo, blk, k, ps)
+        seen = []
+        for call in calls:
+            for k, m, dsts in call:
+                if k not in seen:
+                    g.wait_ge(T.sem["a%d_%d" % (blk, k)], lands[(core, blk, k)])
+                    seen.append(k)
+            sent += _forward(g, core, T, topo, blk, call)
         g.wait_ge(T.sem.sent, sent)
         return
 
-    half = 4 * 2 * NC
-    g.sync.dma_start(T.wb[:, 0:half], T.w1[:, 0:half]).then_inc(T.sem.ld0, 16)
-    g.scalar.dma_start(T.wb[:, half:2 * half], T.w1[:, half:2 * half]).then_inc(T.sem.ld1, 16)
-    g.sync.dma_start(T.wb[:, 2 * half:4 * BLK], T.w2[:, :]).then_inc(T.sem.ld1, 16)
-    g.scalar.dma_start(T.xb[:, :], T.x[:, :]).then_inc(T.sem.ldx, 16)
+    tw = 4 * NC
+    g.sync.dma_start(T.wb[:, 0:2 * tw], T.w1[:, 0:2 * tw]).then_inc(T.sem.ld0, 16)
+    g.scalar.dma_start(T.wb[:, 2 * tw:3 * tw], T.w1[:, 2 * tw:3 * tw]).then_inc(T.sem.ldm, 16)
+    g.sync.dma_start(T.wb[:, 3 * tw:4 * tw], T.w1[:, 3 * tw:4 * tw]).then_inc(T.sem.ld1, 16)
+    g.scalar.dma_start(T.wb[:, 4 * tw:5 * tw], T.w2[:, :]).then_inc(T.sem.ld1, 16)
+    g.sync.dma_start(T.xb[:, :], T.x[:, :]).then_inc(T.sem.ldx, 16)
 
     s0 = BLK * me
     g.vector.wait_ge(T.sem.ld0, 16)
-    g.vector.quantize_mx(T.wq[:, s0:s0 + 2 * NC], T.ws[:, s0:s0 + 2 * NC], T.wb[:, 0:half]).then_inc(T.sem.q0, 1)
+    g.vector.quantize_mx(T.wq[:, s0:s0 + 2 * NC], T.ws[:, s0:s0 + 2 * NC], T.wb[:, 0:2 * tw]).then_inc(T.sem.q0, 1)
+    g.vector.wait_ge(T.sem.ldm, 16)
+    g.vector.quantize_mx(T.wq[:, s0 + 2 * NC:s0 + 3 * NC], T.ws[:, s0 + 2 * NC:s0 + 3 * NC],
+                         T.wb[:, 2 * tw:3 * tw]).then_inc(T.sem.qm, 1)
     g.vector.wait_ge(T.sem.ld1, 32)
-    g.vector.quantize_mx(T.wq[:, s0 + 2 * NC:s0 + BLK], T.ws[:, s0 + 2 * NC:s0 + BLK],
-                         T.wb[:, half:4 * BLK]).then_inc(T.sem.q1, 1)
+    g.vector.quantize_mx(T.wq[:, s0 + 3 * NC:s0 + BLK], T.ws[:, s0 + 3 * NC:s0 + BLK],
+                         T.wb[:, 3 * tw:5 * tw]).then_inc(T.sem.q1, 1)
     g.vector.wait_ge(T.sem.ldx, 16)
     g.vector.quantize_mx(T.xq[:, :], T.xs[:, :], T.xb[:, :]).then_inc(T.sem.qx, 1)
 
-    g.wait_ge(T.sem.q0, 1)
-    for k, ps in todo:
-        if k == 1:
-            g.wait_ge(T.sem.q1, 1)
-        sent += _forward(g, core, T, topo, blk, k, ps)
+    waited = []
+    for call in calls:
+        for k, m, dsts in call:
+            if READY[k] not in waited:
+                g.wait_ge(T.sem[READY[k]], 1)
+                waited.append(READY[k])
+        sent += _forward(g, core, T, topo, blk, call)
 
     zc, ac, turn = [0] * RING, [0] * RING, [0]
     need = dict((r, []) for r in range(N))
@@ -184,7 +215,7 @@ def rank_program(g, core, T, topo):
 
     def second_layer(r):
         if r != me:
-            landed(r, 3)
+            landed(r, P_W2)
         g.tensor.wait_ge(T.sem["qh%d" % r], 1)
         c0 = BLK * r + G * NC
         g.tensor.matmul_mx(ybank, T.wq[:, c0:c0 + NC], T.ws[:, c0:c0 + NC], T.hq[:, NC * r:NC * (r + 1)],
@@ -192,6 +223,7 @@ def rank_program(g, core, T, topo):
         done[0] += 1
 
     g.tensor.wait_ge(T.sem.q0, 1)
+    g.tensor.wait_ge(T.sem.qm, 1)
     g.tensor.wait_ge(T.sem.q1, 1)
     g.tensor.wait_ge(T.sem.qx, 1)
     for i in range(G):
@@ -200,20 +232,20 @@ def rank_program(g, core, T, topo):
     second_layer(me)
 
     for r in order(core):
-        landed(r, 0)
-        landed(r, 1)
-        first_layer(r, 0)
-        first_layer(r, 1)
-    behind = None
+        landed(r, P_PLANE)
+        for i in range(G - 1):
+            landed(r, P_TILE[i])
+            first_layer(r, i)
+    behind = []
     for r in order(core):
-        landed(r, 2)
-        first_layer(r, 2)
-        first_layer(r, 3)
+        landed(r, P_TILE[G - 1])
+        first_layer(r, G - 1)
         pack(r)
-        if behind is not None:
-            second_layer(behind)
-        behind = r
-    second_layer(behind)
+        behind.append(r)
+        if len(behind) > LAG:
+            second_layer(behind.pop(0))
+    for r in behind:
+        second_layer(r)
 
     g.vector.wait_ge(T.sem.ys, N)
     g.vector.tensor_copy(T.ysb[:, :], ybank).then_inc(T.sem.yc, 1)

from concourse.bass import DstId, RemoteDMATransfer
from concourse.mybir import dt, AluOpType, ActivationFunctionType

N = 8
NC = 128
G = 4
BLK = (G + 1) * NC
PIECES = (("codes", 0, NC, "A"), ("codes", NC, 2 * NC, "B"), ("codes", 2 * NC, 3 * NC, "B"), ("plane", 0, BLK, "A"),
          ("codes", 3 * NC, 4 * NC, "B"), ("codes", 4 * NC, BLK, "A"))
EARLY = 2
READY = ("q0", "q0", "qm", "q1", "q1", "q1")
P_TILE = (0, 1, 2, 4)
P_PLANE, P_W2 = 3, 5
SCALE = 0.023
LAG = 2
RING = 7

SCRATCH = {
    "wb": ("sbuf", [128, 4 * BLK], "bfloat16"),
    "xb": ("sbuf", [128, 4 * NC], "bfloat16"),
    "wq": ("sbuf", [128, N * BLK], "float8_e4m3fn_x4"),
    "ws": ("sbuf", [128, N * BLK], "uint8"),
    "xq": ("sbuf", [128, NC], "float8_e4m3fn_x4"),
    "xs": ("sbuf", [128, NC], "uint8"),
    "h": ("sbuf", [128, N * 4 * NC], "bfloat16"),
    "hq": ("sbuf", [128, N * NC], "float8_e4m3fn_x4"),
    "hs": ("sbuf", [128, N * NC], "uint8"),
    "ysb": ("sbuf", [128, NC], "float32"),
    "z": ("psum", [128, 512 * (RING + 1)], "float32"),
}
SEMAPHORES = (["a%d_%d" % (r, k) for r in range(N) for k in range(len(PIECES))]
              + ["zb%d" % j for j in range(RING)] + ["ab%d" % j for j in range(RING)]
              + ["qh%d" % r for r in range(N)]
              + ["ld0", "ldm", "ld1", "ldx", "q0", "qm", "q1", "qx", "ys", "yc", "st", "sent"])


def _bits(m):
    return bin(m).count("1")


def _deal(m):
    one = [1 << i for i in range(m.bit_length()) if (m >> i) & 1]
    return sum(one[0::2]), sum(one[1::2])


def _plan(T, topo):
    ranks = list(T.cores)
    world = range((max(topo.host(c) for c in ranks) + 1) * topo.CORES_PER_HOST)

    def twin(a):
        return [b for b in ranks if topo.host(b) == topo.host(a) and topo.chip(b) != topo.chip(a)][0]

    def peers(a):
        return [b for b in ranks if b != a and topo.chip(b) == topo.chip(a)]

    def near(a):
        return [b for b in peers(a) if topo.same_plane(a, b)][0]

    def cabled(a):
        return [b for b in peers(a) if topo.may_write(a, b) and not topo.same_plane(a, b)][0]

    hubs = {}
    for a in ranks:
        own = [c for c in world if c != a and topo.host(c) == topo.host(a) and topo.chip(c) == topo.chip(a)
               and topo.may_write(c, twin(a))]
        same = [c for c in own if topo.die(c) == topo.die(a)]
        other = [c for c in own if topo.die(c) != topo.die(a)]
        hubs[a] = {"homeA": same[0], "cableA": same[1], "homeB": other[0], "cableB": other[1]}

    def masks(src, off, on):
        m_off = topo.mask(src, off[0])
        for d in off:
            m_off &= topo.mask(src, d)
        return m_off, topo.mask(src, on) & ~m_off

    jobs = {}
    for r, a in enumerate(ranks):
        s, c = near(a), cabled(a)
        d = near(c)
        m_off, m_on = masks(a, [hubs[c]["cableA"], hubs[c]["cableB"]], hubs[a]["homeA"])
        early = range(EARLY)
        calls = [[(k, m, [hubs[c]["cable" + PIECES[k][3]]]) for k, m in zip(early, _deal(m_off))],
                 [(k, m, [hubs[a]["home" + PIECES[k][3]]]) for k, m in zip(early, _deal(m_on))]]
        for k in range(EARLY, len(PIECES)):
            side = PIECES[k][3]
            calls.append([(k, m_off, [hubs[c]["cable" + side]]), (k, m_on, [hubs[a]["home" + side]])])
        jobs[a] = (r, calls)
        for side in "AB":
            mine = [k for k, p in enumerate(PIECES) if p[3] == side]
            hh, hc = hubs[a]["home" + side], hubs[c]["cable" + side]
            out_h, out_c = [twin(a), s, twin(s)], [twin(c), d, twin(d)]
            mh = masks(hh, out_h, a)[0]
            jobs[hh] = (r, [[(k, mh, out_h)] for k in mine])
            mc_off, mc_on = masks(hc, out_c, c)
            calls = [[(mine[0], mc_off, out_c)], [(mine[0], mc_on, [c])]]
            for k in mine[1:]:
                calls.append([(k, mc_off, out_c), (k, mc_on, [c])])
            jobs[hc] = (r, calls)
    lands = {}
    for src in jobs:
        r, calls = jobs[src]
        for call in calls:
            for k, m, dsts in call:
                for d in dsts:
                    lands[(d, r, k)] = _bits(m)

    def order(v):
        s, c = near(v), cabled(v)
        d = near(c)
        return [ranks.index(b) for b in (twin(v), s, twin(s), c, twin(c), d, twin(d))]

    return jobs, lands, order


def _view(T, r, k):
    kind, lo, hi = PIECES[k][0:3]
    if kind == "codes":
        return T.wq[:, BLK * r + lo:BLK * r + hi].bitcast(dt.uint8)
    return T.ws[:, BLK * r + lo:BLK * r + hi]


def _forward(g, core, T, topo, r, call):
    trs = []
    for k, m, dsts in call:
        ids = []
        for d in dsts:
            rid, pid = topo.addr(d, core)
            ids.append(DstId(rid=rid, pnc=pid))
        trs.append(RemoteDMATransfer(dst_ids=ids, dma_engine_mask=m, remote_sem=T.sem["a%d_%d" % (r, k)],
                                     srcs=[_view(T, r, k)], dsts=[_view(T, r, k) for d in dsts]))
    g.remote_dma_fused(trs, local_sem=T.sem.sent)
    return sum(_bits(m) for k, m, dsts in call)


def rank_program(g, core, T, topo):
    jobs, lands, order = _plan(T, topo)
    if core not in jobs:
        return
    me = T.rank_of(core)
    blk, calls = jobs[core]
    sent = 0

    if me is None:
        seen = []
        for call in calls:
            for k, m, dsts in call:
                if k not in seen:
                    g.wait_ge(T.sem["a%d_%d" % (blk, k)], lands[(core, blk, k)])
                    seen.append(k)
            sent += _forward(g, core, T, topo, blk, call)
        g.wait_ge(T.sem.sent, sent)
        return

    tw = 4 * NC
    g.sync.dma_start(T.wb[:, 0:2 * tw], T.w1[:, 0:2 * tw]).then_inc(T.sem.ld0, 16)
    g.scalar.dma_start(T.wb[:, 2 * tw:3 * tw], T.w1[:, 2 * tw:3 * tw]).then_inc(T.sem.ldm, 16)
    g.sync.dma_start(T.wb[:, 3 * tw:4 * tw], T.w1[:, 3 * tw:4 * tw]).then_inc(T.sem.ld1, 16)
    g.scalar.dma_start(T.wb[:, 4 * tw:5 * tw], T.w2[:, :]).then_inc(T.sem.ld1, 16)
    g.sync.dma_start(T.xb[:, :], T.x[:, :]).then_inc(T.sem.ldx, 16)

    s0 = BLK * me
    g.vector.wait_ge(T.sem.ld0, 16)
    g.vector.quantize_mx(T.wq[:, s0:s0 + 2 * NC], T.ws[:, s0:s0 + 2 * NC], T.wb[:, 0:2 * tw]).then_inc(T.sem.q0, 1)
    g.vector.wait_ge(T.sem.ldm, 16)
    g.vector.quantize_mx(T.wq[:, s0 + 2 * NC:s0 + 3 * NC], T.ws[:, s0 + 2 * NC:s0 + 3 * NC],
                         T.wb[:, 2 * tw:3 * tw]).then_inc(T.sem.qm, 1)
    g.vector.wait_ge(T.sem.ld1, 32)
    g.vector.quantize_mx(T.wq[:, s0 + 3 * NC:s0 + BLK], T.ws[:, s0 + 3 * NC:s0 + BLK],
                         T.wb[:, 3 * tw:5 * tw]).then_inc(T.sem.q1, 1)
    g.vector.wait_ge(T.sem.ldx, 16)
    g.vector.quantize_mx(T.xq[:, :], T.xs[:, :], T.xb[:, :]).then_inc(T.sem.qx, 1)

    waited = []
    for call in calls:
        for k, m, dsts in call:
            if READY[k] not in waited:
                g.wait_ge(T.sem[READY[k]], 1)
                waited.append(READY[k])
        sent += _forward(g, core, T, topo, blk, call)

    zc, ac, turn = [0] * RING, [0] * RING, [0]
    need = dict((r, []) for r in range(N))
    ybank = T.z[:, 512 * RING:512 * RING + NC]

    def landed(r, k):
        g.tensor.wait_ge(T.sem["a%d_%d" % (r, k)], lands[(core, r, k)])

    def first_layer(r, i):
        j = turn[0] % RING
        turn[0] += 1
        bank = T.z[:, 512 * j:512 * j + NC]
        if ac[j]:
            g.tensor.wait_ge(T.sem["ab%d" % j], ac[j])
        c0 = BLK * r + NC * i
        g.tensor.matmul_mx(bank, T.wq[:, c0:c0 + NC], T.ws[:, c0:c0 + NC], T.xq[:, :], T.xs[:, :],
                           True, True).then_inc(T.sem["zb%d" % j], 1)
        zc[j] += 1
        out = T.h[:, 4 * NC * r + i:4 * NC * (r + 1):4]
        if i % 2 == 0:
            g.vector.wait_ge(T.sem["zb%d" % j], zc[j])
            g.vector.tensor_scalar(out, bank, 0.0, SCALE, AluOpType.max, AluOpType.mult).then_inc(T.sem["ab%d" % j], 1)
        else:
            g.scalar.wait_ge(T.sem["zb%d" % j], zc[j])
            g.scalar.activation(out, bank, ActivationFunctionType.Relu, scale=SCALE).then_inc(T.sem["ab%d" % j], 1)
        ac[j] += 1
        need[r].append((j, ac[j]))

    def pack(r):
        for j, n in need[r]:
            g.vector.wait_ge(T.sem["ab%d" % j], n)
        g.vector.quantize_mx(T.hq[:, NC * r:NC * (r + 1)], T.hs[:, NC * r:NC * (r + 1)],
                             T.h[:, 4 * NC * r:4 * NC * (r + 1)]).then_inc(T.sem["qh%d" % r], 1)

    done = [0]

    def second_layer(r):
        if r != me:
            landed(r, P_W2)
        g.tensor.wait_ge(T.sem["qh%d" % r], 1)
        c0 = BLK * r + G * NC
        g.tensor.matmul_mx(ybank, T.wq[:, c0:c0 + NC], T.ws[:, c0:c0 + NC], T.hq[:, NC * r:NC * (r + 1)],
                           T.hs[:, NC * r:NC * (r + 1)], done[0] == 0, done[0] == N - 1).then_inc(T.sem.ys, 1)
        done[0] += 1

    g.tensor.wait_ge(T.sem.q0, 1)
    g.tensor.wait_ge(T.sem.qm, 1)
    g.tensor.wait_ge(T.sem.q1, 1)
    g.tensor.wait_ge(T.sem.qx, 1)
    for i in range(G):
        first_layer(me, i)
    pack(me)
    second_layer(me)

    for r in order(core):
        landed(r, P_PLANE)
        for i in range(G - 1):
            landed(r, P_TILE[i])
            first_layer(r, i)
    behind = []
    for r in order(core):
        landed(r, P_TILE[G - 1])
        first_layer(r, G - 1)
        pack(r)
        behind.append(r)
        if len(behind) > LAG:
            second_layer(behind.pop(0))
    for r in behind:
        second_layer(r)

    g.vector.wait_ge(T.sem.ys, N)
    g.vector.tensor_copy(T.ysb[:, :], ybank).then_inc(T.sem.yc, 1)
    g.sync.wait_ge(T.sem.yc, 1)
    g.sync.dma_start(T.y[:, :], T.ysb[:, :]).then_inc(T.sem.st, 16)
    g.sync.wait_ge(T.sem.st, 16)
    g.wait_ge(T.sem.sent, sent)
